import numpy as np
import ml_dtypes

BF16 = ml_dtypes.bfloat16


def bf(x):
    return np.asarray(x, np.float32).astype(BF16)


def f32(x):
    return np.asarray(x, np.float32)


def f64(x):
    return np.asarray(x).astype(np.float64)


def striped(idx):
    return np.concatenate([l.reshape(-1, 16).T for l in idx])


def rows(idx, k):
    return np.tile(np.repeat(idx, 16, axis=0), (k // (16 * 8), 1))


def look(tab, idx):
    return np.take_along_axis(f64(tab), rows(idx, len(tab)), axis=1)


K, S, D, V, N, M = 128, 2048, 3, 512, 1536, 256


def setup_inputs():
    return {"tab": f32(np.random.standard_normal((K, S))), "x0": f32(np.random.standard_normal((K, V))), "w": bf(np.random.standard_normal((K, M)) / np.sqrt(K)), "offs": striped(np.stack([np.random.permutation(S)[:N] for _ in range(8)]))}


def reference(tab, x0, w, offs):
    idx = np.stack([g.T.reshape(-1) for g in np.split(offs, 8)])
    x = f64(x0)
    for d in range(D):
        x = np.minimum(x, look(tab, idx[:, d * V:(d + 1) * V]))
    y = f64(w).T @ x
    return y

@@ -1,0 +1,51 @@
+import concourse.mybir as mybir
+
+F32, BF16, U16 = mybir.dt.float32, mybir.dt.bfloat16, mybir.dt.uint16
+MIN = mybir.AluOpType.min
+
+P = 128
+S = 2048
+D = 3
+V = 512
+M = 256
+FLOPS = 2 * P * M * V
+
+
+def tile_lookup_pool_min_none_kernel(tc, tab, x0, w, offs, out):
+    nc = tc.nc
+    step = V // 16
+
+    with (
+        tc.tile_pool(name="held", bufs=1) as held,
+        tc.psum_pool(name="psum", bufs=1) as psum,
+    ):
+        lists = held.tile([P, D * step], U16, name="lists")
+        nc.sync.dma_start(lists[:], offs)
+        table = held.tile([P, S], F32, name="table")
+        nc.sync.dma_start(table[:], tab)
+        centre = held.tile([P, V], F32, name="centre")
+        nc.scalar.dma_start(centre[:], x0)
+        weights = held.tile([P, M], BF16, name="weights")
+        nc.scalar.dma_start(weights[:], w)
+
+        smallest = centre
+        for d in range(D):
+            neighbour = table[:].indirect(lists[:, d * step : (d + 1) * step])
+            lower = held.tile([P, V], F32, name=f"lower{d}")
+            nc.vector.tensor_tensor(lower[:], neighbour, smallest[:], MIN)
+            smallest = lower
+
+        rounded = held.tile([P, V], BF16, name="rounded")
+        nc.vector.tensor_copy(rounded[:], smallest[:])
+
+        for m in range(M // P):
+            rows = slice(m * P, (m + 1) * P)
+            product = psum.tile([P, V], F32, name=f"product{m}")
+            nc.tensor.matmul(product[:], weights[:, rows], rounded[:], start=True, stop=True)
+            result = held.tile([P, V], F32, name=f"result{m}")
+            if m % 2 == 0:
+                nc.vector.tensor_copy(result[:], product[:])
+                nc.sync.dma_start(out[rows, :], result[:])
+            else:
+                nc.scalar.copy(result[:], product[:])
+                nc.scalar.dma_start(out[rows, :], result[:])

@@ -8,6 +8,8 @@ S = 2048
 D = 3
 V = 512
 M = 256
+HALVES = 2
+H = V // HALVES
 FLOPS = 2 * P * M * V
 
 
@@ -35,17 +37,18 @@ def tile_lookup_pool_min_none_kernel(tc, tab, x0, w, offs, out):
             nc.vector.tensor_tensor(lower[:], neighbour, smallest[:], MIN)
             smallest = lower
 
-        rounded = held.tile([P, V], BF16, name="rounded")
-        nc.vector.tensor_copy(rounded[:], smallest[:])
-
-        for m in range(M // P):
-            rows = slice(m * P, (m + 1) * P)
-            product = psum.tile([P, V], F32, name=f"product{m}")
-            nc.tensor.matmul(product[:], weights[:, rows], rounded[:], start=True, stop=True)
-            result = held.tile([P, V], F32, name=f"result{m}")
-            if m % 2 == 0:
-                nc.vector.tensor_copy(result[:], product[:])
-                nc.sync.dma_start(out[rows, :], result[:])
-            else:
-                nc.scalar.copy(result[:], product[:])
-                nc.scalar.dma_start(out[rows, :], result[:])
+        for h in range(HALVES):
+            columns = slice(h * H, (h + 1) * H)
+            rounded = held.tile([P, H], BF16, name=f"rounded{h}")
+            nc.vector.tensor_copy(rounded[:], smallest[:, columns])
+            for m in range(M // P):
+                rows = slice(m * P, (m + 1) * P)
+                product = psum.tile([P, H], F32, name=f"product{m}_{h}")
+                nc.tensor.matmul(product[:], weights[:, rows], rounded[:], start=True, stop=True)
+                result = held.tile([P, H], F32, name=f"result{m}_{h}")
+                if m % 2 == 0:
+                    nc.vector.tensor_copy(result[:], product[:])
+                    nc.sync.dma_start(out[rows, columns], result[:])
+                else:
+                    nc.scalar.copy(result[:], product[:])
+                    nc.scalar.dma_start(out[rows, columns], result[:])

@@ -37,14 +37,18 @@ def tile_lookup_pool_min_none_kernel(tc, tab, x0, w, offs, out):
             nc.vector.tensor_tensor(lower[:], neighbour, smallest[:], MIN)
             smallest = lower
 
+        rounded = []
+        for h in range(HALVES):
+            part = held.tile([P, H], BF16, name=f"rounded{h}")
+            nc.vector.tensor_copy(part[:], smallest[:, h * H : (h + 1) * H])
+            rounded.append(part)
+
         for h in range(HALVES):
             columns = slice(h * H, (h + 1) * H)
-            rounded = held.tile([P, H], BF16, name=f"rounded{h}")
-            nc.vector.tensor_copy(rounded[:], smallest[:, columns])
             for m in range(M // P):
                 rows = slice(m * P, (m + 1) * P)
                 product = psum.tile([P, H], F32, name=f"product{m}_{h}")
-                nc.tensor.matmul(product[:], weights[:, rows], rounded[:], start=True, stop=True)
+                nc.tensor.matmul(product[:], weights[:, rows], rounded[h][:], start=True, stop=True)
                 result = held.tile([P, H], F32, name=f"result{m}_{h}")
                 if m % 2 == 0:
                     nc.vector.tensor_copy(result[:], product[:])

import concourse.mybir as mybir

F32, BF16, U16 = mybir.dt.float32, mybir.dt.bfloat16, mybir.dt.uint16
MIN = mybir.AluOpType.min

P = 128
S = 2048
D = 3
V = 512
M = 256
HALVES = 2
H = V // HALVES
FLOPS = 2 * P * M * V


def tile_lookup_pool_min_none_kernel(tc, tab, x0, w, offs, out):
    nc = tc.nc
    step = V // 16

    with (
        tc.tile_pool(name="held", bufs=1) as held,
        tc.psum_pool(name="psum", bufs=1) as psum,
    ):
        lists = held.tile([P, D * step], U16, name="lists")
        nc.sync.dma_start(lists[:], offs)
        table = held.tile([P, S], F32, name="table")
        nc.sync.dma_start(table[:], tab)
        centre = held.tile([P, V], F32, name="centre")
        nc.scalar.dma_start(centre[:], x0)
        weights = held.tile([P, M], BF16, name="weights")
        nc.scalar.dma_start(weights[:], w)

        smallest = centre
        for d in range(D):
            neighbour = table[:].indirect(lists[:, d * step : (d + 1) * step])
            lower = held.tile([P, V], F32, name=f"lower{d}")
            nc.vector.tensor_tensor(lower[:], neighbour, smallest[:], MIN)
            smallest = lower

        rounded = []
        for h in range(HALVES):
            part = held.tile([P, H], BF16, name=f"rounded{h}")
            nc.vector.tensor_copy(part[:], smallest[:, h * H : (h + 1) * H])
            rounded.append(part)

        for h in range(HALVES):
            columns = slice(h * H, (h + 1) * H)
            for m in range(M // P):
                rows = slice(m * P, (m + 1) * P)
                product = psum.tile([P, H], F32, name=f"product{m}_{h}")
                nc.tensor.matmul(product[:], weights[:, rows], rounded[h][:], start=True, stop=True)
                result = held.tile([P, H], F32, name=f"result{m}_{h}")
                if m % 2 == 0:
                    nc.vector.tensor_copy(result[:], product[:])
                    nc.sync.dma_start(out[rows, columns], result[:])
                else:
                    nc.scalar.copy(result[:], product[:])
                    nc.scalar.dma_start(out[rows, columns], result[:])
